import numpy as np
CORES = [0,1,2,3]
N = 4
def setup_inputs(rng):
    return {"x": rng.standard_normal((N, 128, 1024), dtype=np.float32)}
def reference(x):
    s = x.max(axis=0)
    return {"y": np.broadcast_to(s, (N,) + s.shape)}

from concourse.bass import DstId, RemoteDMATransfer

NB = 4
W = 256

SCRATCH = {
    "xs": ("dram", [NB, 128, W], "float32"),
    "gath": ("dram", [NB, 128, W], "float32"),
    "res": ("dram", [NB, 128, W], "float32"),
}
SEMAPHORES = ["loaded", "sent", "arrived", "res0", "res1", "res2", "res3", "stored"]

MAX = 2


def rank_program(g, core, T, topo):
    ranks = list(T.cores)
    reducers = [4, 5, 6, 7]

    def dst_id(c):
        rid, pid, _se = topo.addr(c)
        return DstId(rid=rid, pnc=pid)

    rank = T.rank_of(core)
    if rank is not None:
        rows = 128 // NB
        g.dma_start(T.xs[:], T.x[:]).then_inc(T.sem.loaded, 16)
        g.wait_ge(T.sem.loaded, 16)
        g.remote_dma_fused(
            [RemoteDMATransfer(dst_ids=[dst_id(reducers[j])], dma_engine_mask=0xF << (4 * j),
                               remote_sem=T.sem.arrived, src=T.xs[j], dst=T.gath[rank])
             for j in range(NB)],
            local_sem=T.sem.sent)
        for j in range(NB):
            q = g.sync if j % 2 == 0 else g.scalar
            q.wait_ge(T.sem["res%d" % j], 16)
            q.dma_start(T.y[j * rows:(j + 1) * rows, :], T.res[j]).then_inc(T.sem.stored, 16)
        g.wait_ge(T.sem.sent, 16)
        g.wait_ge(T.sem.stored, 16 * NB)
    elif core in reducers:
        j = reducers.index(core)
        g.wait_ge(T.sem.arrived, 4 * NB)
        g.remote_dma_fused(
            [RemoteDMATransfer(dst_ids=[dst_id(c) for c in ranks], dma_engine_mask=0xFFFF,
                               remote_sem=T.sem["res%d" % j],
                               srcs=[T.gath[r] for r in range(NB)],
                               dsts=[T.res[j] for _c in ranks], alu_op=MAX)],
            local_sem=T.sem.sent)
        g.wait_ge(T.sem.sent, 16)
